import numpy as np
import ml_dtypes


def mxq(x, axis, fmt="e4m3"):
    dtype, down = {"e4m3": (ml_dtypes.float8_e4m3fn, 7), "e5m2": (ml_dtypes.float8_e5m2, 14)}[fmt]
    v = np.moveaxis(np.asarray(x, np.float32).astype(ml_dtypes.bfloat16).astype(np.float64), axis, -1)
    blocks = v.reshape(v.shape[:-1] + (-1, 32))
    amax = np.abs(blocks).max(-1, keepdims=True)
    byte = np.maximum(np.where(amax > 0, np.frexp(amax)[1] - 1 + 127, 0) - down, 1)
    scale = np.exp2(byte - 127.0)
    codes = (blocks / scale).astype(np.float32).astype(dtype).astype(np.float64)
    return np.moveaxis((codes * scale).reshape(v.shape), -1, axis)


WIDE = False


def mx_kscale(k):
    if not WIDE:
        return np.ones(k)
    levels = np.array([10, -10, 5, -5, 0])
    if k % 512:
        return np.exp2(np.random.permutation(np.resize(levels, k // 32))).repeat(32)
    a = np.empty((k // 512, 16))
    for p in range(k // 512):
        a[p, :8] = np.random.permutation(np.resize(levels, 8))
        for g in range(8):
            far = levels[np.abs(levels - a[p, g]) >= 10]
            a[p, g + 8] = far[np.random.randint(len(far))]
    return np.exp2(a.ravel()).repeat(32)


def f64(x):
    return np.asarray(x).astype(np.float64)


def striped(idx):
    return np.tile(idx.reshape(-1, 16).T, (8, 1)).astype(np.uint16)


def unstriped(offs):
    return offs[:16].T.reshape(-1).astype(np.int64)


def striped8(idx):
    return np.concatenate([x.reshape(-1, 16).T for x in idx]).astype(np.uint16)


def runs(offs, k):
    lists = np.stack([offs[16 * r : 16 * r + 16].T.reshape(-1) for r in range(8)]).astype(np.int64)
    return lists[np.arange(k) % 512 // 64]


def pack_weight(w):
    k, n = w.shape
    w = f64(np.asarray(w, np.float32).astype(ml_dtypes.bfloat16)).reshape(k // 32, 32, n)
    amax = np.abs(w).max(1)
    byte = np.clip(np.where(amax > 0, np.frexp(amax)[1] - 1 + 127 - 7, 1), 1, 254)
    scaled = (w * np.exp2(127.0 - byte)[:, None, :]).reshape(k, n).astype(np.float32)
    words = np.ascontiguousarray(scaled.reshape(k // 512, 128, 4, n).transpose(0, 1, 3, 2)).astype(ml_dtypes.float8_e4m3fn).view(np.uint8)
    return words, np.ascontiguousarray(byte.astype(np.uint8).reshape(k // 512, 16, n))


def unpack_weight(words, scales):
    g, p, n, _ = words.shape
    vals = np.ascontiguousarray(words).view(ml_dtypes.float8_e4m3fn).astype(np.float64) * np.repeat(np.exp2(scales.astype(np.float64) - 127.0), 8, axis=1)[..., None]
    return vals.transpose(0, 1, 3, 2).reshape(g * 512, n)

def planes(y):
    n, m = y.shape
    v = y.astype(np.float32).astype(ml_dtypes.bfloat16).astype(np.float64).reshape(n // 32, 32, m)
    top = np.abs(v).max(1)
    byte = np.clip(np.where(top > 0, np.frexp(top)[1] - 1 + 127 - 7, 1), 1, 254)
    codes = (v * np.exp2(127.0 - byte)[:, None, :]).reshape(n, m).astype(np.float32).astype(ml_dtypes.float8_e4m3fn).view(np.uint8)
    words = codes.reshape(n // 512, 128, 4, m).transpose(0, 1, 3, 2)
    return np.ascontiguousarray(words), np.ascontiguousarray(byte.astype(np.uint8).reshape(n // 512, 16, m))


K, T, S, N, G, H = 512, 2048, 512, 512, 2048, 512


def setup_inputs():
    n = np.random.standard_normal
    s = mx_kscale(K)[:, None]
    u = mx_kscale(H)
    packed_xT = pack_weight(n((K, T)) * s)
    packed_dT = pack_weight(n((K, G)) / s)
    packed_w1 = pack_weight(n((H, N)) / np.sqrt(H) / u[:, None])
    return {
        "x_words": packed_xT[0],
        "x_scales": packed_xT[1],
        "d_words": packed_dT[0],
        "d_scales": packed_dT[1],
        "gn": (np.random.uniform(0.5, 1.5, (H, 1)) * u[:, None]).astype(np.float32),
        "w1_words": packed_w1[0],
        "w1_scales": packed_w1[1],
        "offs": striped(np.random.permutation(T)[:S]),
        "kidx": striped8(np.random.randint(0, G, (8, H))),
    }


def reference(x_words, x_scales, d_words, d_scales, gn, w1_words, w1_scales, offs, kidx):
    d_kidx = unpack_weight(d_words, d_scales)[np.arange(K)[:, None], runs(kidx, K)]
    xq = unpack_weight(x_words, x_scales)[:, unstriped(offs)]
    s = 0.03125 * (d_kidx.T @ xq)
    e = np.exp(s - s.max(axis=1, keepdims=True))
    p = e / e.sum(axis=1, keepdims=True)
    z = f64(gn) * (64.0 * p)
    out_0 = unpack_weight(w1_words, w1_scales).T @ mxq(z, 0, "e4m3")
    return (out_0,) + planes(out_0)

@@ -1,0 +1,220 @@
+from contextlib import ExitStack
+
+import concourse.mybir as mybir
+
+K, T, S, N, G, H = 512, 2048, 512, 512, 2048, 512
+FLOPS = 2 * K * H * S + 2 * H * N * S
+
+F32 = mybir.dt.float32
+BF16 = mybir.dt.bfloat16
+I32 = mybir.dt.int32
+U32 = mybir.dt.uint32
+U16 = mybir.dt.uint16
+U8 = mybir.dt.uint8
+FP8X4 = mybir.dt.float8_e4m3fn_x4
+ALU = mybir.AluOpType
+ACT = mybir.ActivationFunctionType
+
+P = 128
+PACK = 4
+QUAD = 32
+BANK = 512
+SCORE_SCALE = 0.03125
+PROB_SCALE = 64.0
+CHUNKS = (128, 128, 128, 128)
+
+
+def deal(engine, dst, src):
+    engine.tensor_copy(
+        out=dst.rearrange("p (t a i) -> p a t i", t=PACK, i=4),
+        in_=src.rearrange("p (a i t) -> p a t i", t=PACK, i=4),
+    )
+
+
+def weave(nc, dst, src, run):
+    nc.vector.tensor_copy(
+        out=dst.rearrange("p (a i) t -> p a t i", i=run),
+        in_=src.rearrange("p t (a i) -> p a t i", i=run),
+    )
+
+
+def tile_picked_coattn_none_po_kernel(
+    tc, x_words, x_scales, d_words, d_scales, gn, w1_words, w1_scales, offs, kidx, out_0, out_1, out_2
+):
+    nc = tc.nc
+    with ExitStack() as ctx:
+        keep = ctx.enter_context(tc.tile_pool(name="keep", bufs=1))
+        psum = ctx.enter_context(tc.psum_pool(name="psum", bufs=1))
+
+        def words(ap):
+            return ap[0].rearrange("p n t -> p (n t)").bitcast(I32)
+
+        kidx_t = keep.tile([P, H // 16], U16, name="kidx_t")
+        offs_t = keep.tile([P, S // 16], U16, name="offs_t")
+        dw_all = keep.tile([P, G], U32, name="dw_all", tag="dw_all", align_bytes=64)
+        xw_all = keep.tile([P, T], U32, name="xw_all", tag="xw_all", align_bytes=64)
+        ds_all = keep.tile([P, G], U8, name="ds_all", align_bytes=64)
+        xs_all = keep.tile([P, T], U8, name="xs_all", tag="xs_all", align_bytes=64)
+        w1w_raw = keep.tile([P, N], U32, name="w1w_raw", align_bytes=64)
+        warm_in = keep.tile([P, 1], F32, name="warm_in")
+        warm_out = keep.tile([P, 1], F32, name="warm_out")
+
+        nc.vector.memset(ds_all[:].bitcast(I32), 0)
+        nc.vector.memset(xs_all[:].bitcast(I32), 0)
+        nc.vector.memset(warm_in[:], 0.0)
+
+        nc.sync.dma_start(kidx_t[:], kidx)
+        nc.sync.dma_start(offs_t[:], offs)
+        gn_t = keep.tile([P, PACK], F32, name="gn_t")
+        nc.sync.dma_start(gn_t[:], gn.rearrange("(p t) o -> p (t o)", t=PACK))
+        nc.sync.dma_start(dw_all[:].bitcast(I32), words(d_words))
+        nc.sync.dma_start(xw_all[:].bitcast(I32), words(x_words))
+        nc.sync.dma_start(w1w_raw[:].bitcast(I32), words(w1_words))
+
+        nc.scalar.dma_start(ds_all[0:P:8, :].bitcast(I32), d_scales[0].bitcast(I32))
+        for q in range(4):
+            queue = nc.scalar if q < 2 else nc.gpsimd
+            queue.dma_start(
+                xs_all[QUAD * q : QUAD * q + 4, :].bitcast(I32), x_scales[0, 4 * q : 4 * q + 4, :].bitcast(I32)
+            )
+        nc.scalar.activation(warm_out[:], warm_in[:], ACT.Exp)
+
+        ds_pick = keep.tile([P, H], U8, name="ds_pick", align_bytes=64)
+        ds = keep.tile([P, H], U8, name="ds", align_bytes=64)
+        dw_pick = keep.tile([P, H], U32, name="dw_pick", align_bytes=64)
+        dw = keep.tile([P, H], U32, name="dw", align_bytes=64)
+        xs = keep.tile([P, S], U8, name="xs", align_bytes=64)
+        xw = keep.tile([P, S], U32, name="xw", align_bytes=64)
+        w1s = keep.tile([P, N], U8, name="w1s", align_bytes=64)
+        gain = keep.tile([P, PACK], F32, name="gain")
+
+        nc.vector.tensor_copy(ds_pick[:], ds_all[:].indirect(kidx_t[:]))
+        deal(nc.vector, ds[:], ds_pick[:])
+        for r in range(1, 4):
+            nc.scalar.dma_start(ds[r:P:QUAD, :].bitcast(I32), ds[8 * r : P : QUAD, :].bitcast(I32))
+        nc.vector.tensor_copy(xs[:], xs_all[:].indirect(offs_t[:]))
+        nc.vector.tensor_copy(dw_pick[:], dw_all[:].indirect(kidx_t[:]))
+        deal(nc.vector, dw[:], dw_pick[:])
+        half = S // 2
+        for h in range(2):
+            nc.vector.tensor_copy(
+                xw[:, h * half : (h + 1) * half], xw_all[:].indirect(offs_t[:, h * half // 16 : (h + 1) * half // 16])
+            )
+        w1s_raw = keep.tile([P, N], U8, name="w1s_raw", tag="xs_all", align_bytes=64)
+        w1w = keep.tile([P, N], U32, name="w1w", tag="xw_all", align_bytes=64)
+        nc.gpsimd.memset(w1s_raw[:].bitcast(I32), 0)
+        for q in range(4):
+            nc.sync.dma_start(
+                w1s_raw[QUAD * q : QUAD * q + 4, :].bitcast(I32), w1_scales[0, 4 * q : 4 * q + 4, :].bitcast(I32)
+            )
+        deal(nc.gpsimd, w1w[:], w1w_raw[:])
+        deal(nc.gpsimd, w1s[:], w1s_raw[:])
+        nc.gpsimd.tensor_scalar(gain[:], gn_t[:], PROB_SCALE, 0.0, ALU.mult, ALU.add)
+
+        def mx(out, lw, ls, rw, rs):
+            nc.tensor.matmul_mx(
+                out=out, lhsT=lw.bitcast(FP8X4), lhsT_scale=ls, rhs=rw.bitcast(FP8X4), rhs_scale=rs, start=True, stop=True
+            )
+
+        neg = keep.tile([P, PACK, S], F32, name="neg")
+        e = keep.tile([P, PACK, S], F32, name="e")
+        low = keep.tile([P, PACK], F32, name="low")
+        low_first = keep.tile([P, 1], F32, name="low_first")
+        total = keep.tile([P, PACK], F32, name="total")
+        inv = keep.tile([P, PACK], F32, name="inv")
+        z = keep.tile([P, PACK, S], BF16, name="z", align_bytes=64)
+
+        for t in range(PACK):
+            keys = slice(P * t, P * (t + 1))
+            so_far = None
+            if t == 0:
+                cols = slice(0, half)
+                first = psum.tile([P, half], F32, name="first", tag="first")
+                mx(first[:], dw[:, keys], ds[:, keys], xw[:, cols], xs[:, cols])
+                nc.vector.tensor_scalar(
+                    neg[:, t, cols], first[:], -SCORE_SCALE, None, ALU.mult, ALU.min, accum_out=low_first[:]
+                )
+                so_far = low_first[:]
+            cols = slice(half if t == 0 else 0, S)
+            score = psum.tile([P, cols.stop - cols.start], F32, name=f"score{t}")
+            mx(score[:], dw[:, keys], ds[:, keys], xw[:, cols], xs[:, cols])
+            nc.vector.tensor_scalar(
+                neg[:, t, cols], score[:], -SCORE_SCALE, so_far, ALU.mult, ALU.min, accum_out=low[:, t : t + 1]
+            )
+            nc.scalar.activation(
+                e[:, t, :], neg[:, t, :], ACT.Exp, bias=low[:, t : t + 1], scale=-1.0, accum_out=total[:, t : t + 1]
+            )
+
+        factor = keep.tile([P, PACK], F32, name="factor")
+        rest = slice(CHUNKS[0], S)
+        nc.vector.reciprocal(inv[:, 0:2], total[:, 0:2])
+        for t in range(2):
+            nc.vector.tensor_scalar(
+                z[:, t, rest], e[:, t, rest], inv[:, t : t + 1], gain[:, t : t + 1], ALU.mult, ALU.mult
+            )
+        nc.vector.reciprocal(inv[:, 2:3], total[:, 2:3])
+        nc.vector.tensor_tensor(factor[:, 0:3], inv[:, 0:3], gain[:, 0:3], ALU.mult)
+        nc.vector.reciprocal(inv[:, 3:4], total[:, 3:4])
+        nc.vector.tensor_tensor(factor[:, 3:4], inv[:, 3:4], gain[:, 3:4], ALU.mult)
+        for t in range(2, PACK):
+            nc.scalar.activation(z[:, t, rest], e[:, t, rest], ACT.Copy, scale=factor[:, t : t + 1])
+
+        zw = keep.tile([P, S], U32, name="zw", align_bytes=64)
+        zs = keep.tile([P, S], U8, name="zs", align_bytes=64)
+        ow = keep.tile([P, S], U32, name="ow", align_bytes=64)
+        osc = keep.tile([P, S], U8, name="osc", align_bytes=64)
+        out_rows = out_0.rearrange("(p t) j -> p t j", t=PACK)
+        out_words = words(out_1)
+
+        starts = [sum(CHUNKS[:c]) for c in range(len(CHUNKS))]
+        spans = [slice(a, a + w) for a, w in zip(starts, CHUNKS)]
+        woven = []
+        for c, cols in enumerate(spans):
+            zb = keep.tile([P, CHUNKS[c], PACK], BF16, name=f"zb{c}", align_bytes=64)
+            woven.append(zb)
+
+        def quantise(dst_w, dst_s, cols, src):
+            nc.vector.quantize_mx(
+                out=dst_w[:, cols].bitcast(FP8X4), scales=dst_s[:, cols], in_=src[:].rearrange("p c t -> p (c t)")
+            )
+
+        nc.vector.tensor_tensor(
+            woven[0][:].rearrange("p (a i) t -> p a t i", i=2),
+            e[:, :, spans[0]].rearrange("p t (a i) -> p a t i", i=2),
+            factor[:].unsqueeze(1).unsqueeze(3).broadcast_to([P, CHUNKS[0] // 2, PACK, 2]),
+            ALU.mult,
+        )
+        for c, cols in enumerate(spans):
+            if c + 1 < len(spans):
+                weave(nc, woven[c + 1][:], z[:, :, spans[c + 1]], 4)
+            quantise(zw, zs, cols, woven[c])
+
+        results = []
+        for c, cols in enumerate(spans):
+            width = CHUNKS[c]
+            per_bank = BANK // width
+            res = keep.tile([P, PACK, width], F32, name=f"res{c}")
+            for b in range(PACK // per_bank):
+                acc = psum.tile([P, per_bank, width], F32, name=f"acc{c}_{b}", tag="first" if c == 0 else f"acc{c}_{b}")
+                ts = slice(b * per_bank, (b + 1) * per_bank)
+                for u in range(per_bank):
+                    rows = slice(P * (b * per_bank + u), P * (b * per_bank + u + 1))
+                    mx(acc[:, u, :], w1w[:, rows], w1s[:, rows], zw[:, cols], zs[:, cols])
+                nc.scalar.copy(res[:, ts, :], acc[:])
+                nc.sync.dma_start(out_rows[:, ts, cols], res[:, ts, :])
+            results.append(res)
+
+        rounded = []
+        for c, cols in enumerate(spans):
+            ob = keep.tile([P, CHUNKS[c], PACK], BF16, name=f"ob{c}", align_bytes=64)
+            rounded.append(ob)
+            weave(nc, ob[:], results[c][:], 2)
+            quantise(ow, osc, cols, ob)
+            if cols.stop % half == 0:
+                done = slice(cols.stop - half, cols.stop)
+                nc.sync.dma_start(out_words[:, done], ow[:, done].bitcast(I32))
+        for q in range(4):
+            queue = nc.scalar if q % 2 else nc.sync
+            queue.dma_start(
+                out_2[0, 4 * q : 4 * q + 4, :].bitcast(I32), osc[QUAD * q : QUAD * q + 4, :].bitcast(I32)
+            )

@@ -21,6 +21,7 @@ QUAD = 32
 BANK = 512
 SCORE_SCALE = 0.03125
 PROB_SCALE = 64.0
+HEAD = 512
 CHUNKS = (128, 128, 128, 128)
 
 
@@ -31,8 +32,8 @@ def deal(engine, dst, src):
     )
 
 
-def weave(nc, dst, src, run):
-    nc.vector.tensor_copy(
+def weave(copy, dst, src, run):
+    copy(
         out=dst.rearrange("p (a i) t -> p a t i", i=run),
         in_=src.rearrange("p t (a i) -> p a t i", i=run),
     )
@@ -51,62 +52,68 @@ def tile_picked_coattn_none_po_kernel(
 
         kidx_t = keep.tile([P, H // 16], U16, name="kidx_t")
         offs_t = keep.tile([P, S // 16], U16, name="offs_t")
-        dw_all = keep.tile([P, G], U32, name="dw_all", tag="dw_all", align_bytes=64)
-        xw_all = keep.tile([P, T], U32, name="xw_all", tag="xw_all", align_bytes=64)
         ds_all = keep.tile([P, G], U8, name="ds_all", align_bytes=64)
-        xs_all = keep.tile([P, T], U8, name="xs_all", tag="xs_all", align_bytes=64)
+        xs_all = keep.tile([P, T], U8, name="xs_all", align_bytes=64)
+        dw_all = keep.tile([P, G], U32, name="dw_all", align_bytes=64)
+        xw_all = keep.tile([P, T], U32, name="xw_all", tag="xw_all", align_bytes=64)
         w1w_raw = keep.tile([P, N], U32, name="w1w_raw", align_bytes=64)
-        warm_in = keep.tile([P, 1], F32, name="warm_in")
-        warm_out = keep.tile([P, 1], F32, name="warm_out")
+        w1s_raw = keep.tile([P, N], U8, name="w1s_raw", align_bytes=64)
+        gn_t = keep.tile([P, PACK], F32, name="gn_t")
 
+        xs = keep.tile([P, S], U8, name="xs", align_bytes=64)
         nc.vector.memset(ds_all[:].bitcast(I32), 0)
         nc.vector.memset(xs_all[:].bitcast(I32), 0)
-        nc.vector.memset(warm_in[:], 0.0)
+        nc.vector.memset(xs[:].bitcast(I32), 0)
+        nc.vector.memset(w1s_raw[:].bitcast(I32), 0)
 
         nc.sync.dma_start(kidx_t[:], kidx)
+        nc.sync.dma_start(dw_all[:, :HEAD].bitcast(I32), words(d_words)[:, :HEAD])
         nc.sync.dma_start(offs_t[:], offs)
-        gn_t = keep.tile([P, PACK], F32, name="gn_t")
-        nc.sync.dma_start(gn_t[:], gn.rearrange("(p t) o -> p (t o)", t=PACK))
-        nc.sync.dma_start(dw_all[:].bitcast(I32), words(d_words))
+        nc.sync.dma_start(ds_all[0:P:8, :].bitcast(I32), d_scales[0].bitcast(I32))
+        nc.sync.dma_start(xs_all[0:P:8, :].bitcast(I32), x_scales[0].bitcast(I32))
+        nc.sync.dma_start(dw_all[:, HEAD:].bitcast(I32), words(d_words)[:, HEAD:])
         nc.sync.dma_start(xw_all[:].bitcast(I32), words(x_words))
-        nc.sync.dma_start(w1w_raw[:].bitcast(I32), words(w1_words))
-
-        nc.scalar.dma_start(ds_all[0:P:8, :].bitcast(I32), d_scales[0].bitcast(I32))
-        for q in range(4):
-            queue = nc.scalar if q < 2 else nc.gpsimd
-            queue.dma_start(
-                xs_all[QUAD * q : QUAD * q + 4, :].bitcast(I32), x_scales[0, 4 * q : 4 * q + 4, :].bitcast(I32)
-            )
-        nc.scalar.activation(warm_out[:], warm_in[:], ACT.Exp)
 
         ds_pick = keep.tile([P, H], U8, name="ds_pick", align_bytes=64)
         ds = keep.tile([P, H], U8, name="ds", align_bytes=64)
         dw_pick = keep.tile([P, H], U32, name="dw_pick", align_bytes=64)
         dw = keep.tile([P, H], U32, name="dw", align_bytes=64)
-        xs = keep.tile([P, S], U8, name="xs", align_bytes=64)
+        xs_pick = keep.tile([P, S], U8, name="xs_pick", align_bytes=64)
         xw = keep.tile([P, S], U32, name="xw", align_bytes=64)
         w1s = keep.tile([P, N], U8, name="w1s", align_bytes=64)
         gain = keep.tile([P, PACK], F32, name="gain")
 
-        nc.vector.tensor_copy(ds_pick[:], ds_all[:].indirect(kidx_t[:]))
-        deal(nc.vector, ds[:], ds_pick[:])
+        def pick_and_deal(dst, picked, table):
+            for h in range(2):
+                nc.vector.tensor_copy(
+                    picked[:, h * 256 : (h + 1) * 256], table[:].indirect(kidx_t[:, h * 16 : (h + 1) * 16])
+                )
+            for h in range(2):
+                nc.vector.tensor_copy(
+                    out=dst[:].rearrange("p (t h a i) -> p h a t i", t=PACK, h=2, i=4)[:, h],
+                    in_=picked[:, h * 256 : (h + 1) * 256].rearrange("p (a i t) -> p a t i", t=PACK, i=4),
+                )
+
+        pick_and_deal(ds, ds_pick, ds_all)
         for r in range(1, 4):
             nc.scalar.dma_start(ds[r:P:QUAD, :].bitcast(I32), ds[8 * r : P : QUAD, :].bitcast(I32))
-        nc.vector.tensor_copy(xs[:], xs_all[:].indirect(offs_t[:]))
-        nc.vector.tensor_copy(dw_pick[:], dw_all[:].indirect(kidx_t[:]))
-        deal(nc.vector, dw[:], dw_pick[:])
+        nc.vector.tensor_copy(xs_pick[:], xs_all[:].indirect(offs_t[:]))
+        for r in range(4):
+            queue = nc.scalar if r < 2 else nc.sync
+            queue.dma_start(xs[r:P:QUAD, :].bitcast(I32), xs_pick[8 * r : P : QUAD, :].bitcast(I32))
+        nc.sync.dma_start(gn_t[:], gn.rearrange("(p t) o -> p (t o)", t=PACK))
+        nc.sync.dma_start(w1w_raw[:].bitcast(I32), words(w1_words))
+        for q in range(4):
+            nc.sync.dma_start(
+                w1s_raw[QUAD * q : QUAD * q + 4, :].bitcast(I32), w1_scales[0, 4 * q : 4 * q + 4, :].bitcast(I32)
+            )
+        pick_and_deal(dw, dw_pick, dw_all)
         half = S // 2
         for h in range(2):
             nc.vector.tensor_copy(
                 xw[:, h * half : (h + 1) * half], xw_all[:].indirect(offs_t[:, h * half // 16 : (h + 1) * half // 16])
             )
-        w1s_raw = keep.tile([P, N], U8, name="w1s_raw", tag="xs_all", align_bytes=64)
         w1w = keep.tile([P, N], U32, name="w1w", tag="xw_all", align_bytes=64)
-        nc.gpsimd.memset(w1s_raw[:].bitcast(I32), 0)
-        for q in range(4):
-            nc.sync.dma_start(
-                w1s_raw[QUAD * q : QUAD * q + 4, :].bitcast(I32), w1_scales[0, 4 * q : 4 * q + 4, :].bitcast(I32)
-            )
         deal(nc.gpsimd, w1w[:], w1w_raw[:])
         deal(nc.gpsimd, w1s[:], w1s_raw[:])
         nc.gpsimd.tensor_scalar(gain[:], gn_t[:], PROB_SCALE, 0.0, ALU.mult, ALU.add)
@@ -119,28 +126,24 @@ def tile_picked_coattn_none_po_kernel(
         neg = keep.tile([P, PACK, S], F32, name="neg")
         e = keep.tile([P, PACK, S], F32, name="e")
         low = keep.tile([P, PACK], F32, name="low")
-        low_first = keep.tile([P, 1], F32, name="low_first")
+        low_first = keep.tile([P, 2], F32, name="low_first")
         total = keep.tile([P, PACK], F32, name="total")
         inv = keep.tile([P, PACK], F32, name="inv")
         z = keep.tile([P, PACK, S], BF16, name="z", align_bytes=64)
 
-        for t in range(PACK):
+        def score(t, cols, tag, so_far, lowest):
             keys = slice(P * t, P * (t + 1))
-            so_far = None
-            if t == 0:
-                cols = slice(0, half)
-                first = psum.tile([P, half], F32, name="first", tag="first")
-                mx(first[:], dw[:, keys], ds[:, keys], xw[:, cols], xs[:, cols])
-                nc.vector.tensor_scalar(
-                    neg[:, t, cols], first[:], -SCORE_SCALE, None, ALU.mult, ALU.min, accum_out=low_first[:]
-                )
-                so_far = low_first[:]
-            cols = slice(half if t == 0 else 0, S)
-            score = psum.tile([P, cols.stop - cols.start], F32, name=f"score{t}")
-            mx(score[:], dw[:, keys], ds[:, keys], xw[:, cols], xs[:, cols])
-            nc.vector.tensor_scalar(
-                neg[:, t, cols], score[:], -SCORE_SCALE, so_far, ALU.mult, ALU.min, accum_out=low[:, t : t + 1]
-            )
+            bank = psum.tile([P, cols.stop - cols.start], F32, name=tag, tag=tag)
+            mx(bank[:], dw[:, keys], ds[:, keys], xw[:, cols], xs[:, cols])
+            nc.vector.tensor_scalar(neg[:, t, cols], bank[:], -SCORE_SCALE, so_far, ALU.mult, ALU.min, accum_out=lowest)
+
+        for t in range(2):
+            score(t, slice(0, half), f"first{t}", None, low_first[:, t : t + 1])
+        for t in range(PACK):
+            if t < 2:
+                score(t, slice(half, S), f"score{t}", low_first[:, t : t + 1], low[:, t : t + 1])
+            else:
+                score(t, slice(0, S), f"score{t}", None, low[:, t : t + 1])
             nc.scalar.activation(
                 e[:, t, :], neg[:, t, :], ACT.Exp, bias=low[:, t : t + 1], scale=-1.0, accum_out=total[:, t : t + 1]
             )
@@ -184,10 +187,13 @@ def tile_picked_coattn_none_po_kernel(
             factor[:].unsqueeze(1).unsqueeze(3).broadcast_to([P, CHUNKS[0] // 2, PACK, 2]),
             ALU.mult,
         )
-        for c, cols in enumerate(spans):
-            if c + 1 < len(spans):
-                weave(nc, woven[c + 1][:], z[:, :, spans[c + 1]], 4)
-            quantise(zw, zs, cols, woven[c])
+        weave(nc.scalar.copy, woven[2][:], z[:, :, spans[2]], 4)
+        weave(nc.vector.tensor_copy, woven[1][:], z[:, :, spans[1]], 4)
+        for c in (0, 1):
+            quantise(zw, zs, spans[c], woven[c])
+        weave(nc.vector.tensor_copy, woven[3][:], z[:, :, spans[3]], 4)
+        for c in (2, 3):
+            quantise(zw, zs, spans[c], woven[c])
 
         results = []
         for c, cols in enumerate(spans):
@@ -195,7 +201,7 @@ def tile_picked_coattn_none_po_kernel(
             per_bank = BANK // width
             res = keep.tile([P, PACK, width], F32, name=f"res{c}")
             for b in range(PACK // per_bank):
-                acc = psum.tile([P, per_bank, width], F32, name=f"acc{c}_{b}", tag="first" if c == 0 else f"acc{c}_{b}")
+                acc = psum.tile([P, per_bank, width], F32, name=f"acc{c}_{b}", tag=f"first{c}" if c < 2 else f"acc{c}_{b}")
                 ts = slice(b * per_bank, (b + 1) * per_bank)
                 for u in range(per_bank):
                     rows = slice(P * (b * per_bank + u), P * (b * per_bank + u + 1))
@@ -208,10 +214,10 @@ def tile_picked_coattn_none_po_kernel(
         for c, cols in enumerate(spans):
             ob = keep.tile([P, CHUNKS[c], PACK], BF16, name=f"ob{c}", align_bytes=64)
             rounded.append(ob)
-            weave(nc, ob[:], results[c][:], 2)
+            weave(nc.vector.tensor_copy, ob[:], results[c][:], 4)
             quantise(ow, osc, cols, ob)
-            if cols.stop % half == 0:
-                done = slice(cols.stop - half, cols.stop)
+            if c >= 2:
+                done = slice(0 if c == 2 else cols.start, cols.stop)
                 nc.sync.dma_start(out_words[:, done], ow[:, done].bitcast(I32))
         for q in range(4):
             queue = nc.scalar if q % 2 else nc.sync

@@ -136,6 +136,7 @@ def tile_picked_coattn_none_po_kernel(
             bank = psum.tile([P, cols.stop - cols.start], F32, name=tag, tag=tag)
             mx(bank[:], dw[:, keys], ds[:, keys], xw[:, cols], xs[:, cols])
             nc.vector.tensor_scalar(neg[:, t, cols], bank[:], -SCORE_SCALE, so_far, ALU.mult, ALU.min, accum_out=lowest)
+            return bank
 
         for t in range(2):
             score(t, slice(0, half), f"first{t}", None, low_first[:, t : t + 1])
@@ -143,9 +144,21 @@ def tile_picked_coattn_none_po_kernel(
             if t < 2:
                 score(t, slice(half, S), f"score{t}", low_first[:, t : t + 1], low[:, t : t + 1])
             else:
-                score(t, slice(0, S), f"score{t}", None, low[:, t : t + 1])
+                bank = score(t, slice(0, S), f"score{t}", None, low[:, t : t + 1])
+            source, scale = (bank[:], SCORE_SCALE) if t == PACK - 1 else (neg[:, t, :], -1.0)
             nc.scalar.activation(
-                e[:, t, :], neg[:, t, :], ACT.Exp, bias=low[:, t : t + 1], scale=-1.0, accum_out=total[:, t : t + 1]
+                e[:, t, :], source, ACT.Exp, bias=low[:, t : t + 1], scale=scale, accum_out=total[:, t : t + 1]
+            )
+        warm = psum.tile([P, S], F32, name="warm", tag="score3")
+        for u in range(2):
+            nc.tensor.matmul_mx(
+                out=warm[:],
+                lhsT=dw[:, 0:P].bitcast(FP8X4),
+                lhsT_scale=ds[:, 0:P],
+                rhs=xw[:].bitcast(FP8X4),
+                rhs_scale=xs[:],
+                start=(u == 0),
+                stop=(u == 1),
             )
 
         factor = keep.tile([P, PACK], F32, name="factor")

from contextlib import ExitStack

import concourse.mybir as mybir

K, T, S, N, G, H = 512, 2048, 512, 512, 2048, 512
FLOPS = 2 * K * H * S + 2 * H * N * S

F32 = mybir.dt.float32
BF16 = mybir.dt.bfloat16
I32 = mybir.dt.int32
U32 = mybir.dt.uint32
U16 = mybir.dt.uint16
U8 = mybir.dt.uint8
FP8X4 = mybir.dt.float8_e4m3fn_x4
ALU = mybir.AluOpType
ACT = mybir.ActivationFunctionType

P = 128
PACK = 4
QUAD = 32
BANK = 512
SCORE_SCALE = 0.03125
PROB_SCALE = 64.0
HEAD = 512
CHUNKS = (128, 128, 128, 128)


def deal(engine, dst, src):
    engine.tensor_copy(
        out=dst.rearrange("p (t a i) -> p a t i", t=PACK, i=4),
        in_=src.rearrange("p (a i t) -> p a t i", t=PACK, i=4),
    )


def weave(copy, dst, src, run):
    copy(
        out=dst.rearrange("p (a i) t -> p a t i", i=run),
        in_=src.rearrange("p t (a i) -> p a t i", i=run),
    )


def tile_picked_coattn_none_po_kernel(
    tc, x_words, x_scales, d_words, d_scales, gn, w1_words, w1_scales, offs, kidx, out_0, out_1, out_2
):
    nc = tc.nc
    with ExitStack() as ctx:
        keep = ctx.enter_context(tc.tile_pool(name="keep", bufs=1))
        psum = ctx.enter_context(tc.psum_pool(name="psum", bufs=1))

        def words(ap):
            return ap[0].rearrange("p n t -> p (n t)").bitcast(I32)

        kidx_t = keep.tile([P, H // 16], U16, name="kidx_t")
        offs_t = keep.tile([P, S // 16], U16, name="offs_t")
        ds_all = keep.tile([P, G], U8, name="ds_all", align_bytes=64)
        xs_all = keep.tile([P, T], U8, name="xs_all", align_bytes=64)
        dw_all = keep.tile([P, G], U32, name="dw_all", align_bytes=64)
        xw_all = keep.tile([P, T], U32, name="xw_all", tag="xw_all", align_bytes=64)
        w1w_raw = keep.tile([P, N], U32, name="w1w_raw", align_bytes=64)
        w1s_raw = keep.tile([P, N], U8, name="w1s_raw", align_bytes=64)
        gn_t = keep.tile([P, PACK], F32, name="gn_t")

        xs = keep.tile([P, S], U8, name="xs", align_bytes=64)
        nc.vector.memset(ds_all[:].bitcast(I32), 0)
        nc.vector.memset(xs_all[:].bitcast(I32), 0)
        nc.vector.memset(xs[:].bitcast(I32), 0)
        nc.vector.memset(w1s_raw[:].bitcast(I32), 0)

        nc.sync.dma_start(kidx_t[:], kidx)
        nc.sync.dma_start(dw_all[:, :HEAD].bitcast(I32), words(d_words)[:, :HEAD])
        nc.sync.dma_start(offs_t[:], offs)
        nc.sync.dma_start(ds_all[0:P:8, :].bitcast(I32), d_scales[0].bitcast(I32))
        nc.sync.dma_start(xs_all[0:P:8, :].bitcast(I32), x_scales[0].bitcast(I32))
        nc.sync.dma_start(dw_all[:, HEAD:].bitcast(I32), words(d_words)[:, HEAD:])
        nc.sync.dma_start(xw_all[:].bitcast(I32), words(x_words))

        ds_pick = keep.tile([P, H], U8, name="ds_pick", align_bytes=64)
        ds = keep.tile([P, H], U8, name="ds", align_bytes=64)
        dw_pick = keep.tile([P, H], U32, name="dw_pick", align_bytes=64)
        dw = keep.tile([P, H], U32, name="dw", align_bytes=64)
        xs_pick = keep.tile([P, S], U8, name="xs_pick", align_bytes=64)
        xw = keep.tile([P, S], U32, name="xw", align_bytes=64)
        w1s = keep.tile([P, N], U8, name="w1s", align_bytes=64)
        gain = keep.tile([P, PACK], F32, name="gain")

        def pick_and_deal(dst, picked, table):
            for h in range(2):
                nc.vector.tensor_copy(
                    picked[:, h * 256 : (h + 1) * 256], table[:].indirect(kidx_t[:, h * 16 : (h + 1) * 16])
                )
            for h in range(2):
                nc.vector.tensor_copy(
                    out=dst[:].rearrange("p (t h a i) -> p h a t i", t=PACK, h=2, i=4)[:, h],
                    in_=picked[:, h * 256 : (h + 1) * 256].rearrange("p (a i t) -> p a t i", t=PACK, i=4),
                )

        pick_and_deal(ds, ds_pick, ds_all)
        for r in range(1, 4):
            nc.scalar.dma_start(ds[r:P:QUAD, :].bitcast(I32), ds[8 * r : P : QUAD, :].bitcast(I32))
        nc.vector.tensor_copy(xs_pick[:], xs_all[:].indirect(offs_t[:]))
        for r in range(4):
            queue = nc.scalar if r < 2 else nc.sync
            queue.dma_start(xs[r:P:QUAD, :].bitcast(I32), xs_pick[8 * r : P : QUAD, :].bitcast(I32))
        nc.sync.dma_start(gn_t[:], gn.rearrange("(p t) o -> p (t o)", t=PACK))
        nc.sync.dma_start(w1w_raw[:].bitcast(I32), words(w1_words))
        for q in range(4):
            nc.sync.dma_start(
                w1s_raw[QUAD * q : QUAD * q + 4, :].bitcast(I32), w1_scales[0, 4 * q : 4 * q + 4, :].bitcast(I32)
            )
        pick_and_deal(dw, dw_pick, dw_all)
        half = S // 2
        for h in range(2):
            nc.vector.tensor_copy(
                xw[:, h * half : (h + 1) * half], xw_all[:].indirect(offs_t[:, h * half // 16 : (h + 1) * half // 16])
            )
        w1w = keep.tile([P, N], U32, name="w1w", tag="xw_all", align_bytes=64)
        deal(nc.gpsimd, w1w[:], w1w_raw[:])
        deal(nc.gpsimd, w1s[:], w1s_raw[:])
        nc.gpsimd.tensor_scalar(gain[:], gn_t[:], PROB_SCALE, 0.0, ALU.mult, ALU.add)

        def mx(out, lw, ls, rw, rs):
            nc.tensor.matmul_mx(
                out=out, lhsT=lw.bitcast(FP8X4), lhsT_scale=ls, rhs=rw.bitcast(FP8X4), rhs_scale=rs, start=True, stop=True
            )

        neg = keep.tile([P, PACK, S], F32, name="neg")
        e = keep.tile([P, PACK, S], F32, name="e")
        low = keep.tile([P, PACK], F32, name="low")
        low_first = keep.tile([P, 2], F32, name="low_first")
        total = keep.tile([P, PACK], F32, name="total")
        inv = keep.tile([P, PACK], F32, name="inv")
        z = keep.tile([P, PACK, S], BF16, name="z", align_bytes=64)

        def score(t, cols, tag, so_far, lowest):
            keys = slice(P * t, P * (t + 1))
            bank = psum.tile([P, cols.stop - cols.start], F32, name=tag, tag=tag)
            mx(bank[:], dw[:, keys], ds[:, keys], xw[:, cols], xs[:, cols])
            nc.vector.tensor_scalar(neg[:, t, cols], bank[:], -SCORE_SCALE, so_far, ALU.mult, ALU.min, accum_out=lowest)
            return bank

        for t in range(2):
            score(t, slice(0, half), f"first{t}", None, low_first[:, t : t + 1])
        for t in range(PACK):
            if t < 2:
                score(t, slice(half, S), f"score{t}", low_first[:, t : t + 1], low[:, t : t + 1])
            else:
                bank = score(t, slice(0, S), f"score{t}", None, low[:, t : t + 1])
            source, scale = (bank[:], SCORE_SCALE) if t == PACK - 1 else (neg[:, t, :], -1.0)
            nc.scalar.activation(
                e[:, t, :], source, ACT.Exp, bias=low[:, t : t + 1], scale=scale, accum_out=total[:, t : t + 1]
            )
        warm = psum.tile([P, S], F32, name="warm", tag="score3")
        for u in range(2):
            nc.tensor.matmul_mx(
                out=warm[:],
                lhsT=dw[:, 0:P].bitcast(FP8X4),
                lhsT_scale=ds[:, 0:P],
                rhs=xw[:].bitcast(FP8X4),
                rhs_scale=xs[:],
                start=(u == 0),
                stop=(u == 1),
            )

        factor = keep.tile([P, PACK], F32, name="factor")
        rest = slice(CHUNKS[0], S)
        nc.vector.reciprocal(inv[:, 0:2], total[:, 0:2])
        for t in range(2):
            nc.vector.tensor_scalar(
                z[:, t, rest], e[:, t, rest], inv[:, t : t + 1], gain[:, t : t + 1], ALU.mult, ALU.mult
            )
        nc.vector.reciprocal(inv[:, 2:3], total[:, 2:3])
        nc.vector.tensor_tensor(factor[:, 0:3], inv[:, 0:3], gain[:, 0:3], ALU.mult)
        nc.vector.reciprocal(inv[:, 3:4], total[:, 3:4])
        nc.vector.tensor_tensor(factor[:, 3:4], inv[:, 3:4], gain[:, 3:4], ALU.mult)
        for t in range(2, PACK):
            nc.scalar.activation(z[:, t, rest], e[:, t, rest], ACT.Copy, scale=factor[:, t : t + 1])

        zw = keep.tile([P, S], U32, name="zw", align_bytes=64)
        zs = keep.tile([P, S], U8, name="zs", align_bytes=64)
        ow = keep.tile([P, S], U32, name="ow", align_bytes=64)
        osc = keep.tile([P, S], U8, name="osc", align_bytes=64)
        out_rows = out_0.rearrange("(p t) j -> p t j", t=PACK)
        out_words = words(out_1)

        starts = [sum(CHUNKS[:c]) for c in range(len(CHUNKS))]
        spans = [slice(a, a + w) for a, w in zip(starts, CHUNKS)]
        woven = []
        for c, cols in enumerate(spans):
            zb = keep.tile([P, CHUNKS[c], PACK], BF16, name=f"zb{c}", align_bytes=64)
            woven.append(zb)

        def quantise(dst_w, dst_s, cols, src):
            nc.vector.quantize_mx(
                out=dst_w[:, cols].bitcast(FP8X4), scales=dst_s[:, cols], in_=src[:].rearrange("p c t -> p (c t)")
            )

        nc.vector.tensor_tensor(
            woven[0][:].rearrange("p (a i) t -> p a t i", i=2),
            e[:, :, spans[0]].rearrange("p t (a i) -> p a t i", i=2),
            factor[:].unsqueeze(1).unsqueeze(3).broadcast_to([P, CHUNKS[0] // 2, PACK, 2]),
            ALU.mult,
        )
        weave(nc.scalar.copy, woven[2][:], z[:, :, spans[2]], 4)
        weave(nc.vector.tensor_copy, woven[1][:], z[:, :, spans[1]], 4)
        for c in (0, 1):
            quantise(zw, zs, spans[c], woven[c])
        weave(nc.vector.tensor_copy, woven[3][:], z[:, :, spans[3]], 4)
        for c in (2, 3):
            quantise(zw, zs, spans[c], woven[c])

        results = []
        for c, cols in enumerate(spans):
            width = CHUNKS[c]
            per_bank = BANK // width
            res = keep.tile([P, PACK, width], F32, name=f"res{c}")
            for b in range(PACK // per_bank):
                acc = psum.tile([P, per_bank, width], F32, name=f"acc{c}_{b}", tag=f"first{c}" if c < 2 else f"acc{c}_{b}")
                ts = slice(b * per_bank, (b + 1) * per_bank)
                for u in range(per_bank):
                    rows = slice(P * (b * per_bank + u), P * (b * per_bank + u + 1))
                    mx(acc[:, u, :], w1w[:, rows], w1s[:, rows], zw[:, cols], zs[:, cols])
                nc.scalar.copy(res[:, ts, :], acc[:])
                nc.sync.dma_start(out_rows[:, ts, cols], res[:, ts, :])
            results.append(res)

        rounded = []
        for c, cols in enumerate(spans):
            ob = keep.tile([P, CHUNKS[c], PACK], BF16, name=f"ob{c}", align_bytes=64)
            rounded.append(ob)
            weave(nc.vector.tensor_copy, ob[:], results[c][:], 4)
            quantise(ow, osc, cols, ob)
            if c >= 2:
                done = slice(0 if c == 2 else cols.start, cols.stop)
                nc.sync.dma_start(out_words[:, done], ow[:, done].bitcast(I32))
        for q in range(4):
            queue = nc.scalar if q % 2 else nc.sync
            queue.dma_start(
                out_2[0, 4 * q : 4 * q + 4, :].bitcast(I32), osc[QUAD * q : QUAD * q + 4, :].bitcast(I32)
            )
